import numpy as np
import ml_dtypes


def mxq(x, axis, fmt="e4m3"):
    dtype, down = {"e4m3": (ml_dtypes.float8_e4m3fn, 7), "e5m2": (ml_dtypes.float8_e5m2, 14)}[fmt]
    v = np.moveaxis(np.asarray(x, np.float32).astype(ml_dtypes.bfloat16).astype(np.float64), axis, -1)
    blocks = v.reshape(v.shape[:-1] + (-1, 32))
    amax = np.abs(blocks).max(-1, keepdims=True)
    byte = np.maximum(np.where(amax > 0, np.frexp(amax)[1] - 1 + 127, 0) - down, 1)
    scale = np.exp2(byte - 127.0)
    codes = (blocks / scale).astype(np.float32).astype(dtype).astype(np.float64)
    return np.moveaxis((codes * scale).reshape(v.shape), -1, axis)


WIDE = False


def mx_kscale(k):
    if not WIDE:
        return np.ones(k)
    levels = np.array([30, -30])
    if k % 512:
        return np.exp2(np.random.permutation(np.resize(levels, k // 32))).repeat(32)
    a = np.empty((k // 512, 16))
    for p in range(k // 512):
        a[p, :8] = np.random.permutation(np.resize(levels, 8))
        for g in range(8):
            far = levels[np.abs(levels - a[p, g]) >= 10]
            a[p, g + 8] = far[np.random.randint(len(far))]
    return np.exp2(a.ravel()).repeat(32)


BF16 = ml_dtypes.bfloat16


def bf(x):
    return np.asarray(x, np.float32).astype(BF16)


def f64(x):
    return np.asarray(x).astype(np.float64)

E4M3FN = np.array([(-1.0 if i & 128 else 1.0) * ((1.0 + (i & 7) / 8.0) * 2.0 ** (((i >> 3) & 15) - 7) if i & 120 else (i & 7) * 2.0 ** -9) for i in range(256)])


def e4m3fn_bytes(y):
    return np.clip(np.asarray(y, np.float64), -448.0, 448.0).astype(np.float32).astype(ml_dtypes.float8_e4m3fn).view(np.uint8)


def e4m3fn_values(b):
    return E4M3FN[b]

def planes(Y):
    n, m = Y.shape
    b = f64(bf(Y)).reshape(n // 32, 32, m)
    amax = np.abs(b).max(1)
    byte = np.clip(np.where(amax > 0, np.frexp(amax)[1] - 1 + 127 - 7, 1), 1, 254)
    codes = (b * np.exp2(127.0 - byte)[:, None, :]).reshape(n, m).astype(np.float32).astype(ml_dtypes.float8_e4m3fn).view(np.uint8)
    words = codes.reshape(n // 512, 128, 4, m).transpose(0, 1, 3, 2)
    return np.ascontiguousarray(words), np.ascontiguousarray(byte.astype(np.uint8).reshape(n // 512, 16, m))


T, D, F, B = 1024, 1536, 2048, 32

CODE_MAX = 448.0


def setup_inputs():
    s = mx_kscale(D)
    token_size = np.exp(0.8 * np.random.randn(T, 1))
    G = token_size * np.random.randn(T, D) * np.exp(0.8 * np.random.randn(T, D)) * s[None, :]
    G_scale = (np.abs(G).reshape(T, D // B, B).max(axis=2) / CODE_MAX).astype(np.float32)
    G_bytes = e4m3fn_bytes(G / np.repeat(f64(G_scale), B, axis=1))
    w_down = np.random.randn(F, D) / np.sqrt(D) / s[None, :]
    gate = 1.5 * np.random.randn(T, F)
    return {
        "G_bytes": G_bytes,
        "G_scale": G_scale,
        "w_down": bf(w_down),
        "gate": bf(gate),
    }

def reference(G_bytes, G_scale, w_down, gate):
    G = e4m3fn_values(G_bytes) * np.repeat(f64(G_scale), B, axis=1)
    Gq = mxq(G, 1, "e5m2")
    wq = mxq(f64(w_down), 1, "e4m3")
    dh = Gq @ wq.T
    a = f64(gate)
    silu = a / (1.0 + np.exp(-a))
    y = dh * silu
    Y = y
    words, scales = planes(Y)
    return y, words, scales

@@ -1,0 +1,287 @@
+from contextlib import ExitStack
+
+import concourse.mybir as mybir
+from concourse.masks import make_identity
+
+T, D, F = 1024, 1536, 2048
+FLOPS = 2 * T * D * F
+
+F32 = mybir.dt.float32
+BF16 = mybir.dt.bfloat16
+U32 = mybir.dt.uint32
+I32 = mybir.dt.int32
+U8 = mybir.dt.uint8
+FP8 = mybir.dt.float8_e4m3fn
+E4M3X4 = mybir.dt.float8_e4m3fn_x4
+E5M2X4 = mybir.dt.float8_e5m2_x4
+ACT = mybir.ActivationFunctionType
+MULT = mybir.AluOpType.mult
+
+P = 128
+PACK = 4
+K_PASS = P * PACK
+PASSES = D // K_PASS
+BLOCK = 32
+BLOCKS = K_PASS // BLOCK
+GROUP = P * PACK
+GROUPS = T // GROUP
+CHUNK = 512
+CHUNKS = F // CHUNK
+PAIRS = 2
+SPLIT = 256
+SHARE_FROM = 17
+VW = 13
+
+
+def tile_swiglu_up_gradient_tokens_b13_kernel(tc, G_bytes, G_scale, w_down, gate, out_0, out_1, out_2):
+    nc = tc.nc
+    with ExitStack() as ctx:
+        keep = ctx.enter_context(tc.tile_pool(name="keep", bufs=1))
+        work = ctx.enter_context(tc.tile_pool(name="work", bufs=1))
+        psum = ctx.enter_context(tc.psum_pool(name="psum", bufs=8))
+
+        ctx.enter_context(tc.manual_schedule())
+        ident = keep.tile([P, P], F32, name="ident")
+        make_identity(nc, ident[:])
+        warm = keep.tile([P, 1], F32, name="warm")
+        nc.scalar.activation(out=warm[:], in_=ident[:, 0:1], func=ACT.Silu)
+
+        g_rows = G_bytes.rearrange("(g p t) k -> g p (t k)", p=P, t=PACK)
+        s_rows = G_scale.rearrange("(g p t) j -> g p (t j)", p=P, t=PACK)
+        gate_rows = gate.rearrange("(g p t) f -> g p t f", p=P, t=PACK)
+        y_rows = out_0.rearrange("(g p t) f -> g p t f", p=P, t=PACK)
+        code_rows = out_1.rearrange("g p m t -> g p (m t)").bitcast(I32)
+        scale_rows = out_2.bitcast(I32)
+
+        gsc, gbytes, wraw, gates, wfirst = {}, {}, {}, {}, {}
+
+        def load_scales(g):
+            gsc[g] = keep.tile([P, PACK * D // BLOCK], F32, name="gsc%d" % g)
+            nc.sync.dma_start(out=gsc[g][:], in_=s_rows[g])
+
+        def load_g(g, pair):
+            gbytes[g, pair] = keep.tile([P, 2 * D], U8, name="gbytes%d%d" % (g, pair))
+            nc.sync.dma_start(out=gbytes[g, pair][:], in_=g_rows[g][:, pair * 2 * D : (pair + 1) * 2 * D])
+
+        def load_w(c, pair):
+            wraw[c, pair] = keep.tile([P, 2, D], BF16, name="wraw%d%d" % (c, pair))
+            r0 = c * CHUNK + pair * 2 * P
+            nc.sync.dma_start(out=wraw[c, pair][:], in_=w_down[r0 : r0 + 2 * P, :].rearrange("(r p) k -> p r k", p=P))
+
+        def load_w_pass(k):
+            wfirst[k] = keep.tile([P, 4, K_PASS], BF16, name="wfirst%d" % k)
+            nc.sync.dma_start(out=wfirst[k][:], in_=w_down[0:CHUNK, k * K_PASS : (k + 1) * K_PASS].rearrange("(r p) k -> p r k", p=P))
+
+        def load_gate(g, half):
+            gates[g, half] = keep.tile([P, PACK, 2 * CHUNK], BF16, name="gate%d%d" % (g, half))
+            nc.sync.dma_start(out=gates[g, half][:], in_=gate_rows[g][:, :, half * 2 * CHUNK : (half + 1) * 2 * CHUNK])
+
+        load_scales(0)
+        load_g(0, 0)
+        load_w_pass(0)
+        load_w_pass(1)
+        load_g(0, 1)
+        load_w_pass(2)
+        load_w(1, 0)
+        load_gate(0, 0)
+        load_w(1, 1)
+        load_scales(1)
+        load_g(1, 0)
+        load_w(2, 0)
+        load_w(2, 1)
+        load_gate(0, 1)
+        load_g(1, 1)
+        load_w(3, 0)
+        load_w(3, 1)
+        load_gate(1, 0)
+        load_gate(1, 1)
+
+        gq, gs, wq, ws, ys = {}, {}, {}, {}, {}
+        for g in range(GROUPS):
+            ys[g] = keep.tile([P, F], U8, name="yscales%d" % g, align_bytes=64)
+            for pair in range(PAIRS):
+                for k in range(PASSES):
+                    gq[g, pair, k] = keep.tile([P, 2 * P], U32, name="gq%d%d%d" % (g, pair, k), align_bytes=64)
+                    gs[g, pair, k] = keep.tile([P, 2 * P], U8, name="gs%d%d%d" % (g, pair, k), align_bytes=64)
+        for c in range(CHUNKS):
+            for k in range(PASSES):
+                wq[c, k] = keep.tile([P, CHUNK], U32, name="wq%d%d" % (c, k), align_bytes=64)
+                ws[c, k] = keep.tile([P, CHUNK], U8, name="ws%d%d" % (c, k), align_bytes=64)
+
+        words, banks, grouped, accs, silus, ytiles, ygrps = {}, {}, {}, {}, {}, {}, {}
+
+        def widen(unit, r, on_vector):
+            kind, g, pair, k = unit
+            wide = work.tile([P, K_PASS], BF16, name="wide", bufs=12, align_bytes=64)
+            for j in range(BLOCKS):
+                c0 = r * D + k * K_PASS + j * BLOCK
+                src = gbytes[g, pair][:, c0 : c0 + BLOCK].bitcast(FP8)
+                s0 = (2 * pair + r) * (D // BLOCK) + k * BLOCKS + j
+                scale = gsc[g][:, s0 : s0 + 1]
+                dst = wide[:, j * BLOCK : (j + 1) * BLOCK]
+                if not on_vector:
+                    nc.scalar.activation(out=dst, in_=src, func=ACT.Copy, scale=scale)
+                else:
+                    dst = wide[:].rearrange("p (u c e) -> p c u e", u=2, e=2)[:, 8 * j : 8 * j + 8]
+                    src = src.rearrange("p (c u e) -> p c u e", u=2, e=2)
+                    nc.vector.tensor_scalar(out=dst, in0=src, scalar1=scale, scalar2=None, op0=MULT)
+            sorted_words = wide[:].bitcast(F32)
+            words[unit, r] = [sorted_words[:, u * P : (u + 1) * P] if on_vector else sorted_words[:, u : 2 * P : 2] for u in range(2)]
+
+        def turn(unit):
+            kind, c, pair, k = unit
+            if kind == "w":
+                for r in range(2):
+                    rows = wfirst[k][:, 2 * pair + r, :] if c == 0 else wraw[c, pair][:, r, k * K_PASS : (k + 1) * K_PASS]
+                    words[unit, r] = [rows.bitcast(F32)[:, u : 2 * P : 2] for u in range(2)]
+            banks[unit] = psum.tile([P, 512], F32, name="bank")
+            for r in range(2):
+                for u in range(2):
+                    nc.tensor.transpose(banks[unit][:, (2 * r + u) * P : (2 * r + u + 1) * P], words[unit, r][u], ident[:])
+
+        def drain(unit, on_vector):
+            grouped[unit] = work.tile([P, 2 * K_PASS], BF16, name="grp", bufs=8, align_bytes=64)
+            o = grouped[unit][:].bitcast(F32).rearrange("p (r c u) -> p r c u", r=2, u=2)
+            i = banks[unit][:].rearrange("p (r u c) -> p r c u", r=2, u=2)
+            if on_vector:
+                nc.vector.tensor_copy(out=o, in_=i)
+            else:
+                nc.scalar.copy(out=o, in_=i)
+
+        def quantize(unit):
+            kind, g, pair, k = unit
+            if kind == "g":
+                nc.vector.quantize_mx(out=gq[g, pair, k][:].bitcast(E5M2X4), scales=gs[g, pair, k][:], in_=grouped[unit][:])
+            else:
+                cols = slice(pair * 2 * P, (pair + 1) * 2 * P)
+                nc.vector.quantize_mx(out=wq[g, k][:, cols].bitcast(E4M3X4), scales=ws[g, k][:, cols], in_=grouped[unit][:])
+
+        def where(h):
+            return h // (2 * CHUNKS), h // 2 % CHUNKS, h % 2
+
+        def activate(h):
+            g, c, pair = where(h)
+            silus[h] = work.tile([P, 2, CHUNK], F32, name="silu", bufs=4)
+            f0 = (c % 2) * CHUNK
+            nc.scalar.activation(out=silus[h][:], in_=gates[g, c // 2][:, 2 * pair : 2 * pair + 2, f0 : f0 + CHUNK], func=ACT.Silu)
+
+        def multiply(q, k):
+            g, c, pair = where(q // 2)
+            r = q % 2
+            if k == 0:
+                accs[q // 2, r] = psum.tile([P, 512], F32, name="bank")
+            nc.tensor.matmul_mx(
+                out=accs[q // 2, r][:],
+                lhsT=gq[g, pair, k][:, r * P : (r + 1) * P].bitcast(E5M2X4),
+                lhsT_scale=gs[g, pair, k][:, r * P : (r + 1) * P],
+                rhs=wq[c, k][:].bitcast(E4M3X4),
+                rhs_scale=ws[c, k][:],
+                start=(k == 0),
+                stop=(k == PASSES - 1),
+            )
+
+        def product(h, r):
+            g, c, pair = where(h)
+            if pair == 0 and r == 0:
+                ytiles[g, c] = work.tile([P, PACK, CHUNK], F32, name="y", bufs=4)
+            nc.vector.tensor_tensor(out=ytiles[g, c][:, 2 * pair + r, :], in0=accs[h, r][:], in1=silus[h][:, r, :], op=MULT)
+
+        def store_y(h):
+            g, c, pair = where(h)
+            nc.sync.dma_start(out=y_rows[g][:, 2 * pair : 2 * pair + 2, c * CHUNK : (c + 1) * CHUNK], in_=ytiles[g, c][:, 2 * pair : 2 * pair + 2, :])
+
+        def interleave(h, split, on_vector):
+            g, c, pair = where(h)
+            if (g, c) not in ygrps:
+                ygrps[g, c] = work.tile([P, CHUNK, PACK], BF16, name="ygrp", bufs=2, align_bytes=64)
+            dst = ygrps[g, c][:].rearrange("p (c i) t -> p c t i", i=4)
+            src = ytiles[g, c][:].rearrange("p t (c i) -> p c t i", i=4)
+            n = split // 4
+            if on_vector and n > 0:
+                nc.vector.tensor_copy(out=dst[:, :n], in_=src[:, :n])
+            if not on_vector and split < CHUNK:
+                nc.scalar.copy(out=dst[:, n:], in_=src[:, n:])
+
+        def requantize(h):
+            g, c, pair = where(h)
+            cols = slice(c * CHUNK, (c + 1) * CHUNK)
+            ycodes = work.tile([P, CHUNK], U32, name="ycodes", bufs=3, align_bytes=64)
+            nc.vector.quantize_mx(out=ycodes[:].bitcast(E4M3X4), scales=ys[g][:, cols], in_=ygrps[g, c][:].rearrange("p c t -> p (c t)"))
+            nc.sync.dma_start(out=code_rows[g][:, cols], in_=ycodes[:].bitcast(I32))
+            if c == CHUNKS - 1:
+                for q in range(4):
+                    nc.sync.dma_start(out=scale_rows[g][4 * q : 4 * q + 4, :], in_=ys[g][32 * q : 32 * q + 4, :].bitcast(I32))
+
+        def g_units(g, pair):
+            return [("g", g, pair, k) for k in range(PASSES)]
+
+        def w_units(c):
+            return [("w", c, pair, k) for k in range(PASSES) for pair in range(PAIRS)]
+
+        QUARTERS = PACK * GROUPS * CHUNKS
+        g00, g01, g1 = g_units(0, 0), g_units(0, 1), g_units(1, 0) + g_units(1, 1)
+        w0, w1 = w_units(0), w_units(1)
+
+        def both(unit):
+            widen(unit, 0, False)
+            widen(unit, 1, True)
+
+        head = [[g00[k]] + w0[2 * k : 2 * k + 2] for k in range(PASSES)] + [g01[:2] + w1[:1], g01[2:] + w1[1:3]]
+        to_widen = g00 + g01
+        both(to_widen[0])
+        both(to_widen[1])
+        for a, units in enumerate(head):
+            for unit in units:
+                turn(unit)
+            if a > 0:
+                for unit in head[a - 1]:
+                    quantize(unit)
+            if 1 <= a <= 3:
+                multiply(0, a - 1)
+                multiply(1, a - 1)
+            if a == 3:
+                activate(0)
+            if a + 2 < len(to_widen):
+                both(to_widen[a + 2])
+            drain(units[0], False)
+            drain(units[1], a < 3)
+            drain(units[2], False)
+        activate(1)
+        product(0, 0)
+
+        turns = {q: [] for q in range(QUARTERS + 8)}
+        turns[1] = head[-1]
+        turns[2] = w1[3:]
+        later = w_units(2) + w_units(3) + g1
+        for n in range(len(later) // 2):
+            turns[3 + 3 * (n // 2) + n % 2] = later[2 * n : 2 * n + 2]
+        halves = [(unit, r) for unit in g1 for r in range(2)]
+
+        for q in range(2, QUARTERS + 3):
+            for unit in turns[q]:
+                turn(unit)
+            done = (q - 5) // 4 * 2 + 1
+            split = CHUNK if q < SHARE_FROM else SPLIT
+            if q % 4 == 1 and q >= 5:
+                interleave(done, split, True)
+            if q >= 3 and halves and q % 4 in (3, 0) and q < VW:
+                widen(*halves.pop(0), True)
+            if q - 1 < QUARTERS:
+                product((q - 1) // 2, (q - 1) % 2)
+                if q % 2 == 0:
+                    store_y((q - 1) // 2)
+            if q % 4 == 2 and q >= 6:
+                requantize(done)
+            for unit in turns[q - 1]:
+                quantize(unit)
+            if q < QUARTERS:
+                for k in range(PASSES):
+                    multiply(q, k)
+            if q % 2 == 0 and q // 2 + 1 < QUARTERS // 2:
+                activate(q // 2 + 1)
+            if q >= 3 and halves and q % 2 == 1:
+                widen(*halves.pop(0), False)
+            for unit in turns[q]:
+                drain(unit, False)
+            if q % 4 == 0 and q >= 4:
+                interleave((q - 4) // 4 * 2 + 1, CHUNK if q + 1 < SHARE_FROM else SPLIT, False)

@@ -16,6 +16,7 @@ E4M3X4 = mybir.dt.float8_e4m3fn_x4
 E5M2X4 = mybir.dt.float8_e5m2_x4
 ACT = mybir.ActivationFunctionType
 MULT = mybir.AluOpType.mult
+ADD = mybir.AluOpType.add
 
 P = 128
 PACK = 4
@@ -28,9 +29,19 @@ GROUPS = T // GROUP
 CHUNK = 512
 CHUNKS = F // CHUNK
 PAIRS = 2
-SPLIT = 256
-SHARE_FROM = 17
-VW = 13
+WB = 12
+HV = 5
+RQ = 2
+VQ = [4,8,12]
+SQ = [5,6,7,9,10,11,13]
+DV = []
+SH = [(512,512)]*3+[(256,512)]*4+[(344,512)]
+GF = 0
+Z0 = 0
+ZA = []
+HVW = [4,5]
+HS = []
+TQ = [4,5,6,8,9,10,12,13,14]
 
 
 def tile_swiglu_up_gradient_tokens_b13_kernel(tc, G_bytes, G_scale, w_down, gate, out_0, out_1, out_2):
@@ -43,8 +54,10 @@ def tile_swiglu_up_gradient_tokens_b13_kernel(tc, G_bytes, G_scale, w_down, gate
         ctx.enter_context(tc.manual_schedule())
         ident = keep.tile([P, P], F32, name="ident")
         make_identity(nc, ident[:])
+        seed = keep.tile([P, 1], F32, name="seed")
+        nc.vector.memset(seed[:], 0.0)
         warm = keep.tile([P, 1], F32, name="warm")
-        nc.scalar.activation(out=warm[:], in_=ident[:, 0:1], func=ACT.Silu)
+        nc.scalar.activation(out=warm[:], in_=seed[:], func=ACT.Silu)
 
         g_rows = G_bytes.rearrange("(g p t) k -> g p (t k)", p=P, t=PACK)
         s_rows = G_scale.rearrange("(g p t) j -> g p (t j)", p=P, t=PACK)
@@ -53,7 +66,7 @@ def tile_swiglu_up_gradient_tokens_b13_kernel(tc, G_bytes, G_scale, w_down, gate
         code_rows = out_1.rearrange("g p m t -> g p (m t)").bitcast(I32)
         scale_rows = out_2.bitcast(I32)
 
-        gsc, gbytes, wraw, gates, wfirst = {}, {}, {}, {}, {}
+        gsc, gbytes, wraw, gates, wfirst, gfirst = {}, {}, {}, {}, {}, {}
 
         def load_scales(g):
             gsc[g] = keep.tile([P, PACK * D // BLOCK], F32, name="gsc%d" % g)
@@ -63,10 +76,17 @@ def tile_swiglu_up_gradient_tokens_b13_kernel(tc, G_bytes, G_scale, w_down, gate
             gbytes[g, pair] = keep.tile([P, 2 * D], U8, name="gbytes%d%d" % (g, pair))
             nc.sync.dma_start(out=gbytes[g, pair][:], in_=g_rows[g][:, pair * 2 * D : (pair + 1) * 2 * D])
 
+        def load_g_first():
+            gfirst[0] = keep.tile([P, 2, K_PASS], U8, name="gfirst0")
+            gfirst[1] = keep.tile([P, 2, D - K_PASS], U8, name="gfirst1")
+            rows = g_rows[0][:, : 2 * D].rearrange("p (r k) -> p r k", r=2)
+            nc.sync.dma_start(out=gfirst[0][:], in_=rows[:, :, :K_PASS])
+            nc.sync.dma_start(out=gfirst[1][:], in_=rows[:, :, K_PASS:])
+
         def load_w(c, pair):
             wraw[c, pair] = keep.tile([P, 2, D], BF16, name="wraw%d%d" % (c, pair))
             r0 = c * CHUNK + pair * 2 * P
-            nc.sync.dma_start(out=wraw[c, pair][:], in_=w_down[r0 : r0 + 2 * P, :].rearrange("(r p) k -> p r k", p=P))
+            nc.sync.dma_start(out=wraw[c, pair][:], in_=w_down[r0 : r0 + 2 * P, :].rearrange("(p r) k -> p r k", r=2))
 
         def load_w_pass(k):
             wfirst[k] = keep.tile([P, 4, K_PASS], BF16, name="wfirst%d" % k)
@@ -77,7 +97,10 @@ def tile_swiglu_up_gradient_tokens_b13_kernel(tc, G_bytes, G_scale, w_down, gate
             nc.sync.dma_start(out=gates[g, half][:], in_=gate_rows[g][:, :, half * 2 * CHUNK : (half + 1) * 2 * CHUNK])
 
         load_scales(0)
-        load_g(0, 0)
+        if GF:
+            load_g_first()
+        else:
+            load_g(0, 0)
         load_w_pass(0)
         load_w_pass(1)
         load_g(0, 1)
@@ -89,8 +112,8 @@ def tile_swiglu_up_gradient_tokens_b13_kernel(tc, G_bytes, G_scale, w_down, gate
         load_g(1, 0)
         load_w(2, 0)
         load_w(2, 1)
-        load_gate(0, 1)
         load_g(1, 1)
+        load_gate(0, 1)
         load_w(3, 0)
         load_w(3, 1)
         load_gate(1, 0)
@@ -112,10 +135,14 @@ def tile_swiglu_up_gradient_tokens_b13_kernel(tc, G_bytes, G_scale, w_down, gate
 
         def widen(unit, r, on_vector):
             kind, g, pair, k = unit
-            wide = work.tile([P, K_PASS], BF16, name="wide", bufs=12, align_bytes=64)
+            wide = work.tile([P, K_PASS], BF16, name="wide", bufs=WB, align_bytes=64)
             for j in range(BLOCKS):
                 c0 = r * D + k * K_PASS + j * BLOCK
-                src = gbytes[g, pair][:, c0 : c0 + BLOCK].bitcast(FP8)
+                if GF and g == 0 and pair == 0:
+                    c1 = j * BLOCK + max(k - 1, 0) * K_PASS
+                    src = gfirst[min(k, 1)][:, r, c1 : c1 + BLOCK].bitcast(FP8)
+                else:
+                    src = gbytes[g, pair][:, c0 : c0 + BLOCK].bitcast(FP8)
                 s0 = (2 * pair + r) * (D // BLOCK) + k * BLOCKS + j
                 scale = gsc[g][:, s0 : s0 + 1]
                 dst = wide[:, j * BLOCK : (j + 1) * BLOCK]
@@ -140,9 +167,10 @@ def tile_swiglu_up_gradient_tokens_b13_kernel(tc, G_bytes, G_scale, w_down, gate
                     nc.tensor.transpose(banks[unit][:, (2 * r + u) * P : (2 * r + u + 1) * P], words[unit, r][u], ident[:])
 
         def drain(unit, on_vector):
-            grouped[unit] = work.tile([P, 2 * K_PASS], BF16, name="grp", bufs=8, align_bytes=64)
-            o = grouped[unit][:].bitcast(F32).rearrange("p (r c u) -> p r c u", r=2, u=2)
-            i = banks[unit][:].rearrange("p (r u c) -> p r c u", r=2, u=2)
+            grouped[unit] = work.tile([P, 2 * K_PASS], BF16, name="grp", bufs=6, align_bytes=64)
+            order = "c r u" if unit[0] == "w" and unit[1] > 0 else "r c u"
+            o = grouped[unit][:].bitcast(F32).rearrange("p (%s) -> p %s" % (order, order), r=2, u=2)
+            i = banks[unit][:].rearrange("p (r u c) -> p %s" % order, r=2, u=2)
             if on_vector:
                 nc.vector.tensor_copy(out=o, in_=i)
             else:
@@ -162,13 +190,13 @@ def tile_swiglu_up_gradient_tokens_b13_kernel(tc, G_bytes, G_scale, w_down, gate
         def activate(h):
             g, c, pair = where(h)
             silus[h] = work.tile([P, 2, CHUNK], F32, name="silu", bufs=4)
-            f0 = (c % 2) * CHUNK
-            nc.scalar.activation(out=silus[h][:], in_=gates[g, c // 2][:, 2 * pair : 2 * pair + 2, f0 : f0 + CHUNK], func=ACT.Silu)
+            nc.scalar.activation(out=silus[h][:], in_=gates[g, c // 2][:, 2 * pair : 2 * pair + 2, c % 2 * CHUNK : (c % 2 + 1) * CHUNK], func=ACT.Silu)
 
         def multiply(q, k):
             g, c, pair = where(q // 2)
             r = q % 2
-            if k == 0:
+            first = (q // 2, r) not in accs
+            if first:
                 accs[q // 2, r] = psum.tile([P, 512], F32, name="bank")
             nc.tensor.matmul_mx(
                 out=accs[q // 2, r][:],
@@ -176,31 +204,35 @@ def tile_swiglu_up_gradient_tokens_b13_kernel(tc, G_bytes, G_scale, w_down, gate
                 lhsT_scale=gs[g, pair, k][:, r * P : (r + 1) * P],
                 rhs=wq[c, k][:].bitcast(E4M3X4),
                 rhs_scale=ws[c, k][:],
-                start=(k == 0),
+                start=first,
                 stop=(k == PASSES - 1),
             )
 
         def product(h, r):
             g, c, pair = where(h)
             if pair == 0 and r == 0:
-                ytiles[g, c] = work.tile([P, PACK, CHUNK], F32, name="y", bufs=4)
+                ytiles[g, c] = work.tile([P, PACK, CHUNK], F32, name="y", bufs=3)
             nc.vector.tensor_tensor(out=ytiles[g, c][:, 2 * pair + r, :], in0=accs[h, r][:], in1=silus[h][:, r, :], op=MULT)
 
-        def store_y(h):
-            g, c, pair = where(h)
-            nc.sync.dma_start(out=y_rows[g][:, 2 * pair : 2 * pair + 2, c * CHUNK : (c + 1) * CHUNK], in_=ytiles[g, c][:, 2 * pair : 2 * pair + 2, :])
+        def store_y(q, n):
+            g, c, pair = where(q // 2)
+            t = slice(q % PACK + 1 - n, q % PACK + 1)
+            nc.sync.dma_start(out=y_rows[g][:, t, c * CHUNK : (c + 1) * CHUNK], in_=ytiles[g, c][:, t, :])
 
-        def interleave(h, split, on_vector):
-            g, c, pair = where(h)
+        def interleave(step, engine, c0, c1):
+            g, c = divmod(step, CHUNKS)
+            if c0 == c1:
+                return
             if (g, c) not in ygrps:
                 ygrps[g, c] = work.tile([P, CHUNK, PACK], BF16, name="ygrp", bufs=2, align_bytes=64)
-            dst = ygrps[g, c][:].rearrange("p (c i) t -> p c t i", i=4)
-            src = ytiles[g, c][:].rearrange("p t (c i) -> p c t i", i=4)
-            n = split // 4
-            if on_vector and n > 0:
-                nc.vector.tensor_copy(out=dst[:, :n], in_=src[:, :n])
-            if not on_vector and split < CHUNK:
-                nc.scalar.copy(out=dst[:, n:], in_=src[:, n:])
+            dst = ygrps[g, c][:].rearrange("p (c i) t -> p c t i", i=4)[:, c0 // 4 : c1 // 4]
+            src = ytiles[g, c][:].rearrange("p t (c i) -> p c t i", i=4)[:, c0 // 4 : c1 // 4]
+            if engine == "vector":
+                nc.vector.tensor_copy(out=dst, in_=src)
+            elif engine == "scalar":
+                nc.scalar.copy(out=dst, in_=src)
+            else:
+                nc.gpsimd.tensor_scalar(out=dst, in0=src, scalar1=1.0, scalar2=0.0, op0=MULT, op1=ADD)
 
         def requantize(h):
             g, c, pair = where(h)
@@ -210,7 +242,7 @@ def tile_swiglu_up_gradient_tokens_b13_kernel(tc, G_bytes, G_scale, w_down, gate
             nc.sync.dma_start(out=code_rows[g][:, cols], in_=ycodes[:].bitcast(I32))
             if c == CHUNKS - 1:
                 for q in range(4):
-                    nc.sync.dma_start(out=scale_rows[g][4 * q : 4 * q + 4, :], in_=ys[g][32 * q : 32 * q + 4, :].bitcast(I32))
+                    (nc.scalar if g == GROUPS - 1 else nc.sync).dma_start(out=scale_rows[g][4 * q : 4 * q + 4, :], in_=ys[g][32 * q : 32 * q + 4, :].bitcast(I32))
 
         def g_units(g, pair):
             return [("g", g, pair, k) for k in range(PASSES)]
@@ -221,67 +253,80 @@ def tile_swiglu_up_gradient_tokens_b13_kernel(tc, G_bytes, G_scale, w_down, gate
         QUARTERS = PACK * GROUPS * CHUNKS
         g00, g01, g1 = g_units(0, 0), g_units(0, 1), g_units(1, 0) + g_units(1, 1)
         w0, w1 = w_units(0), w_units(1)
+        halves = [(unit, r) for unit in g1 for r in range(2)]
 
         def both(unit):
             widen(unit, 0, False)
             widen(unit, 1, True)
 
-        head = [[g00[k]] + w0[2 * k : 2 * k + 2] for k in range(PASSES)] + [g01[:2] + w1[:1], g01[2:] + w1[1:3]]
+        head = [[g00[k]] + w0[2 * k : 2 * k + 2] for k in range(PASSES)] + [g01[:2] + w1[:1], g01[2:] + w1[1:3], w1[3:]]
+        passes = [[], [(0, 0)], [(0, 1)], [(0, 2)], [(2, 0), (2, 1)], [(2, 2)]]
         to_widen = g00 + g01
         both(to_widen[0])
         both(to_widen[1])
         for a, units in enumerate(head):
             for unit in units:
                 turn(unit)
+            if a == 5:
+                product(0, 1)
+                store_y(1, 2)
             if a > 0:
                 for unit in head[a - 1]:
                     quantize(unit)
-            if 1 <= a <= 3:
-                multiply(0, a - 1)
-                multiply(1, a - 1)
-            if a == 3:
-                activate(0)
+            for q, k in passes[a]:
+                multiply(q, k)
+                multiply(q + 1, k)
+            if a >= 3:
+                activate(a - 3)
+            if a == 4:
+                product(0, 0)
             if a + 2 < len(to_widen):
                 both(to_widen[a + 2])
+            if a in HVW:
+                widen(*halves.pop(0), True)
             drain(units[0], False)
-            drain(units[1], a < 3)
+            drain(units[1], a < HV)
             drain(units[2], False)
-        activate(1)
-        product(0, 0)
+            if a in HS:
+                widen(*halves.pop(0), False)
 
         turns = {q: [] for q in range(QUARTERS + 8)}
-        turns[1] = head[-1]
-        turns[2] = w1[3:]
+        turns[3] = head[-1]
         later = w_units(2) + w_units(3) + g1
         for n in range(len(later) // 2):
-            turns[3 + 3 * (n // 2) + n % 2] = later[2 * n : 2 * n + 2]
-        halves = [(unit, r) for unit in g1 for r in range(2)]
+            turns[TQ[n]] = later[2 * n : 2 * n + 2]
 
-        for q in range(2, QUARTERS + 3):
+        for q in range(4, QUARTERS + 4):
             for unit in turns[q]:
                 turn(unit)
-            done = (q - 5) // 4 * 2 + 1
-            split = CHUNK if q < SHARE_FROM else SPLIT
-            if q % 4 == 1 and q >= 5:
-                interleave(done, split, True)
-            if q >= 3 and halves and q % 4 in (3, 0) and q < VW:
+            done = (q - 4) // 4 * 2 + 1
+            if q == 4:
+                for unit in turns[3]:
+                    quantize(unit)
+                product(1, 0)
+            if halves and q in VQ:
                 widen(*halves.pop(0), True)
             if q - 1 < QUARTERS:
                 product((q - 1) // 2, (q - 1) % 2)
-                if q % 2 == 0:
-                    store_y((q - 1) // 2)
-            if q % 4 == 2 and q >= 6:
+                if q - 1 >= QUARTERS - 2:
+                    store_y(q - 1, 1)
+                elif q % 2 == 0:
+                    store_y(q - 1, 2)
+            if q % 4 == 1 and q >= 5:
+                interleave(done // 2, "vector", 0, SH[done // 2][0])
+            if q % 4 == RQ and q >= 4 + RQ:
                 requantize(done)
-            for unit in turns[q - 1]:
-                quantize(unit)
+            if q > 4:
+                for unit in turns[q - 1]:
+                    quantize(unit)
             if q < QUARTERS:
                 for k in range(PASSES):
                     multiply(q, k)
             if q % 2 == 0 and q // 2 + 1 < QUARTERS // 2:
                 activate(q // 2 + 1)
-            if q >= 3 and halves and q % 2 == 1:
+            if halves and q in SQ:
                 widen(*halves.pop(0), False)
-            for unit in turns[q]:
-                drain(unit, False)
+            for n, unit in enumerate(turns[q]):
+                drain(unit, (q, n) in DV)
             if q % 4 == 0 and q >= 4:
-                interleave((q - 4) // 4 * 2 + 1, CHUNK if q + 1 < SHARE_FROM else SPLIT, False)
+                interleave(q // 4 - 1, "scalar", SH[q // 4 - 1][0], SH[q // 4 - 1][1])

@@ -16,7 +16,6 @@ E4M3X4 = mybir.dt.float8_e4m3fn_x4
 E5M2X4 = mybir.dt.float8_e5m2_x4
 ACT = mybir.ActivationFunctionType
 MULT = mybir.AluOpType.mult
-ADD = mybir.AluOpType.add
 
 P = 128
 PACK = 4
@@ -24,24 +23,15 @@ K_PASS = P * PACK
 PASSES = D // K_PASS
 BLOCK = 32
 BLOCKS = K_PASS // BLOCK
-GROUP = P * PACK
-GROUPS = T // GROUP
+GROUPS = T // (P * PACK)
 CHUNK = 512
 CHUNKS = F // CHUNK
-PAIRS = 2
-WB = 12
-HV = 5
-RQ = 2
-VQ = [4,8,12]
-SQ = [5,6,7,9,10,11,13]
-DV = []
-SH = [(512,512)]*3+[(256,512)]*4+[(344,512)]
-GF = 0
-Z0 = 0
-ZA = []
-HVW = [4,5]
-HS = []
-TQ = [4,5,6,8,9,10,12,13,14]
+STEPS = GROUPS * CHUNKS
+QUARTERS = PACK * STEPS
+SCALE_ROWS = 4
+
+VECTOR_COLUMNS = 304
+VECTOR_COLUMNS_LAST = 368
 
 
 def tile_swiglu_up_gradient_tokens_b13_kernel(tc, G_bytes, G_scale, w_down, gate, out_0, out_1, out_2):
@@ -50,65 +40,55 @@ def tile_swiglu_up_gradient_tokens_b13_kernel(tc, G_bytes, G_scale, w_down, gate
         keep = ctx.enter_context(tc.tile_pool(name="keep", bufs=1))
         work = ctx.enter_context(tc.tile_pool(name="work", bufs=1))
         psum = ctx.enter_context(tc.psum_pool(name="psum", bufs=8))
-
         ctx.enter_context(tc.manual_schedule())
+
         ident = keep.tile([P, P], F32, name="ident")
         make_identity(nc, ident[:])
-        seed = keep.tile([P, 1], F32, name="seed")
-        nc.vector.memset(seed[:], 0.0)
-        warm = keep.tile([P, 1], F32, name="warm")
-        nc.scalar.activation(out=warm[:], in_=seed[:], func=ACT.Silu)
+        zero = keep.tile([P, 1], F32, name="zero")
+        nc.vector.memset(zero[:], 0.0)
+        zero_bias = keep.tile([P, 1], F32, name="zero_bias")
+        nc.scalar.activation(out=zero_bias[:], in_=zero[:], func=ACT.Silu)
 
         g_rows = G_bytes.rearrange("(g p t) k -> g p (t k)", p=P, t=PACK)
-        s_rows = G_scale.rearrange("(g p t) j -> g p (t j)", p=P, t=PACK)
+        g_scale_rows = G_scale.rearrange("(g p t) j -> g p (t j)", p=P, t=PACK)
         gate_rows = gate.rearrange("(g p t) f -> g p t f", p=P, t=PACK)
         y_rows = out_0.rearrange("(g p t) f -> g p t f", p=P, t=PACK)
-        code_rows = out_1.rearrange("g p m t -> g p (m t)").bitcast(I32)
-        scale_rows = out_2.bitcast(I32)
+        y_code_rows = out_1.rearrange("g p m t -> g p (m t)").bitcast(I32)
+        y_scale_rows = out_2.bitcast(I32)
 
-        gsc, gbytes, wraw, gates, wfirst, gfirst = {}, {}, {}, {}, {}, {}
+        g_scales, g_raw, w_first, w_raw, gates = {}, {}, {}, {}, {}
 
-        def load_scales(g):
-            gsc[g] = keep.tile([P, PACK * D // BLOCK], F32, name="gsc%d" % g)
-            nc.sync.dma_start(out=gsc[g][:], in_=s_rows[g])
+        def load_g_scales(g):
+            g_scales[g] = keep.tile([P, PACK * D // BLOCK], F32, name="g_scales%d" % g)
+            nc.sync.dma_start(out=g_scales[g][:], in_=g_scale_rows[g])
 
         def load_g(g, pair):
-            gbytes[g, pair] = keep.tile([P, 2 * D], U8, name="gbytes%d%d" % (g, pair))
-            nc.sync.dma_start(out=gbytes[g, pair][:], in_=g_rows[g][:, pair * 2 * D : (pair + 1) * 2 * D])
+            g_raw[g, pair] = keep.tile([P, 2 * D], U8, name="g_raw%d%d" % (g, pair))
+            nc.sync.dma_start(out=g_raw[g, pair][:], in_=g_rows[g][:, pair * 2 * D : (pair + 1) * 2 * D])
 
-        def load_g_first():
-            gfirst[0] = keep.tile([P, 2, K_PASS], U8, name="gfirst0")
-            gfirst[1] = keep.tile([P, 2, D - K_PASS], U8, name="gfirst1")
-            rows = g_rows[0][:, : 2 * D].rearrange("p (r k) -> p r k", r=2)
-            nc.sync.dma_start(out=gfirst[0][:], in_=rows[:, :, :K_PASS])
-            nc.sync.dma_start(out=gfirst[1][:], in_=rows[:, :, K_PASS:])
+        def load_w_first(a):
+            w_first[a] = keep.tile([P, PACK, K_PASS], BF16, name="w_first%d" % a)
+            nc.sync.dma_start(out=w_first[a][:], in_=w_down[0:CHUNK, a * K_PASS : (a + 1) * K_PASS].rearrange("(r p) k -> p r k", p=P))
 
         def load_w(c, pair):
-            wraw[c, pair] = keep.tile([P, 2, D], BF16, name="wraw%d%d" % (c, pair))
-            r0 = c * CHUNK + pair * 2 * P
-            nc.sync.dma_start(out=wraw[c, pair][:], in_=w_down[r0 : r0 + 2 * P, :].rearrange("(p r) k -> p r k", r=2))
-
-        def load_w_pass(k):
-            wfirst[k] = keep.tile([P, 4, K_PASS], BF16, name="wfirst%d" % k)
-            nc.sync.dma_start(out=wfirst[k][:], in_=w_down[0:CHUNK, k * K_PASS : (k + 1) * K_PASS].rearrange("(r p) k -> p r k", p=P))
+            w_raw[c, pair] = keep.tile([P, 2, D], BF16, name="w_raw%d%d" % (c, pair))
+            row0 = c * CHUNK + pair * 2 * P
+            nc.sync.dma_start(out=w_raw[c, pair][:], in_=w_down[row0 : row0 + 2 * P, :].rearrange("(p r) k -> p r k", r=2))
 
         def load_gate(g, half):
             gates[g, half] = keep.tile([P, PACK, 2 * CHUNK], BF16, name="gate%d%d" % (g, half))
             nc.sync.dma_start(out=gates[g, half][:], in_=gate_rows[g][:, :, half * 2 * CHUNK : (half + 1) * 2 * CHUNK])
 
-        load_scales(0)
-        if GF:
-            load_g_first()
-        else:
-            load_g(0, 0)
-        load_w_pass(0)
-        load_w_pass(1)
+        load_g_scales(0)
+        load_g(0, 0)
+        load_w_first(0)
+        load_w_first(1)
         load_g(0, 1)
-        load_w_pass(2)
+        load_w_first(2)
         load_w(1, 0)
         load_gate(0, 0)
         load_w(1, 1)
-        load_scales(1)
+        load_g_scales(1)
         load_g(1, 0)
         load_w(2, 0)
         load_w(2, 1)
@@ -119,214 +99,206 @@ def tile_swiglu_up_gradient_tokens_b13_kernel(tc, G_bytes, G_scale, w_down, gate
         load_gate(1, 0)
         load_gate(1, 1)
 
-        gq, gs, wq, ws, ys = {}, {}, {}, {}, {}
+        g_codes, g_mx_scales, w_codes, w_mx_scales, y_mx_scales = {}, {}, {}, {}, {}
         for g in range(GROUPS):
-            ys[g] = keep.tile([P, F], U8, name="yscales%d" % g, align_bytes=64)
-            for pair in range(PAIRS):
-                for k in range(PASSES):
-                    gq[g, pair, k] = keep.tile([P, 2 * P], U32, name="gq%d%d%d" % (g, pair, k), align_bytes=64)
-                    gs[g, pair, k] = keep.tile([P, 2 * P], U8, name="gs%d%d%d" % (g, pair, k), align_bytes=64)
+            y_mx_scales[g] = keep.tile([P, F], U8, name="y_mx_scales%d" % g, align_bytes=64)
+            for pair in range(2):
+                for a in range(PASSES):
+                    g_codes[g, pair, a] = keep.tile([P, 2 * P], U32, name="g_codes%d%d%d" % (g, pair, a), align_bytes=64)
+                    g_mx_scales[g, pair, a] = keep.tile([P, 2 * P], U8, name="g_mx_scales%d%d%d" % (g, pair, a), align_bytes=64)
         for c in range(CHUNKS):
-            for k in range(PASSES):
-                wq[c, k] = keep.tile([P, CHUNK], U32, name="wq%d%d" % (c, k), align_bytes=64)
-                ws[c, k] = keep.tile([P, CHUNK], U8, name="ws%d%d" % (c, k), align_bytes=64)
+            for a in range(PASSES):
+                w_codes[c, a] = keep.tile([P, CHUNK], U32, name="w_codes%d%d" % (c, a), align_bytes=64)
+                w_mx_scales[c, a] = keep.tile([P, CHUNK], U8, name="w_mx_scales%d%d" % (c, a), align_bytes=64)
 
-        words, banks, grouped, accs, silus, ytiles, ygrps = {}, {}, {}, {}, {}, {}, {}
+        pair_words, turned, k_major = {}, {}, {}
 
-        def widen(unit, r, on_vector):
-            kind, g, pair, k = unit
-            wide = work.tile([P, K_PASS], BF16, name="wide", bufs=WB, align_bytes=64)
+        def widen(slab, r, on_vector):
+            operand, g, pair, a = slab
+            wide = work.tile([P, K_PASS], BF16, name="wide", bufs=2 * len(second_group), align_bytes=64)
             for j in range(BLOCKS):
-                c0 = r * D + k * K_PASS + j * BLOCK
-                if GF and g == 0 and pair == 0:
-                    c1 = j * BLOCK + max(k - 1, 0) * K_PASS
-                    src = gfirst[min(k, 1)][:, r, c1 : c1 + BLOCK].bitcast(FP8)
+                byte0 = r * D + a * K_PASS + j * BLOCK
+                values = g_raw[g, pair][:, byte0 : byte0 + BLOCK].bitcast(FP8)
+                column = (2 * pair + r) * (D // BLOCK) + a * BLOCKS + j
+                scale = g_scales[g][:, column : column + 1]
+                if on_vector:
+                    by_u = wide[:].rearrange("p (u w e) -> p w u e", u=2, e=2)[:, 8 * j : 8 * j + 8]
+                    nc.vector.tensor_scalar(out=by_u, in0=values.rearrange("p (w u e) -> p w u e", u=2, e=2), scalar1=scale, scalar2=None, op0=MULT)
                 else:
-                    src = gbytes[g, pair][:, c0 : c0 + BLOCK].bitcast(FP8)
-                s0 = (2 * pair + r) * (D // BLOCK) + k * BLOCKS + j
-                scale = gsc[g][:, s0 : s0 + 1]
-                dst = wide[:, j * BLOCK : (j + 1) * BLOCK]
-                if not on_vector:
-                    nc.scalar.activation(out=dst, in_=src, func=ACT.Copy, scale=scale)
-                else:
-                    dst = wide[:].rearrange("p (u c e) -> p c u e", u=2, e=2)[:, 8 * j : 8 * j + 8]
-                    src = src.rearrange("p (c u e) -> p c u e", u=2, e=2)
-                    nc.vector.tensor_scalar(out=dst, in0=src, scalar1=scale, scalar2=None, op0=MULT)
-            sorted_words = wide[:].bitcast(F32)
-            words[unit, r] = [sorted_words[:, u * P : (u + 1) * P] if on_vector else sorted_words[:, u : 2 * P : 2] for u in range(2)]
+                    nc.scalar.activation(out=wide[:, j * BLOCK : (j + 1) * BLOCK], in_=values, func=ACT.Copy, scale=scale)
+            words = wide[:].bitcast(F32)
+            pair_words[slab, r] = [words[:, u * P : (u + 1) * P] if on_vector else words[:, u : 2 * P : 2] for u in range(2)]
 
-        def turn(unit):
-            kind, c, pair, k = unit
-            if kind == "w":
+        def turn(slab):
+            operand, c, pair, a = slab
+            if operand == "w":
                 for r in range(2):
-                    rows = wfirst[k][:, 2 * pair + r, :] if c == 0 else wraw[c, pair][:, r, k * K_PASS : (k + 1) * K_PASS]
-                    words[unit, r] = [rows.bitcast(F32)[:, u : 2 * P : 2] for u in range(2)]
-            banks[unit] = psum.tile([P, 512], F32, name="bank")
+                    rows = w_first[a][:, 2 * pair + r, :] if c == 0 else w_raw[c, pair][:, r, a * K_PASS : (a + 1) * K_PASS]
+                    pair_words[slab, r] = [rows.bitcast(F32)[:, u : 2 * P : 2] for u in range(2)]
+            turned[slab] = psum.tile([P, CHUNK], F32, name="bank")
             for r in range(2):
                 for u in range(2):
-                    nc.tensor.transpose(banks[unit][:, (2 * r + u) * P : (2 * r + u + 1) * P], words[unit, r][u], ident[:])
+                    nc.tensor.transpose(turned[slab][:, (2 * r + u) * P : (2 * r + u + 1) * P], pair_words[slab, r][u], ident[:])
 
-        def drain(unit, on_vector):
-            grouped[unit] = work.tile([P, 2 * K_PASS], BF16, name="grp", bufs=6, align_bytes=64)
-            order = "c r u" if unit[0] == "w" and unit[1] > 0 else "r c u"
-            o = grouped[unit][:].bitcast(F32).rearrange("p (%s) -> p %s" % (order, order), r=2, u=2)
-            i = banks[unit][:].rearrange("p (r u c) -> p %s" % order, r=2, u=2)
+        def drain(slab, on_vector):
+            k_major[slab] = work.tile([P, 2 * K_PASS], BF16, name="k_major", bufs=6, align_bytes=64)
+            order = "n r u" if slab[0] == "w" and slab[1] > 0 else "r n u"
+            dst = k_major[slab][:].bitcast(F32).rearrange("p (%s) -> p %s" % (order, order), r=2, u=2)
+            src = turned[slab][:].rearrange("p (r u n) -> p %s" % order, r=2, u=2)
             if on_vector:
-                nc.vector.tensor_copy(out=o, in_=i)
+                nc.vector.tensor_copy(out=dst, in_=src)
             else:
-                nc.scalar.copy(out=o, in_=i)
+                nc.scalar.copy(out=dst, in_=src)
 
-        def quantize(unit):
-            kind, g, pair, k = unit
-            if kind == "g":
-                nc.vector.quantize_mx(out=gq[g, pair, k][:].bitcast(E5M2X4), scales=gs[g, pair, k][:], in_=grouped[unit][:])
+        def quantize(slab):
+            operand, index, pair, a = slab
+            if operand == "g":
+                nc.vector.quantize_mx(out=g_codes[index, pair, a][:].bitcast(E5M2X4), scales=g_mx_scales[index, pair, a][:], in_=k_major[slab][:])
             else:
                 cols = slice(pair * 2 * P, (pair + 1) * 2 * P)
-                nc.vector.quantize_mx(out=wq[g, k][:, cols].bitcast(E4M3X4), scales=ws[g, k][:, cols], in_=grouped[unit][:])
+                nc.vector.quantize_mx(out=w_codes[index, a][:, cols].bitcast(E4M3X4), scales=w_mx_scales[index, a][:, cols], in_=k_major[slab][:])
 
-        def where(h):
-            return h // (2 * CHUNKS), h // 2 % CHUNKS, h % 2
+        sums, silus, y_tiles, y_packed = {}, {}, {}, {}
 
-        def activate(h):
-            g, c, pair = where(h)
-            silus[h] = work.tile([P, 2, CHUNK], F32, name="silu", bufs=4)
-            nc.scalar.activation(out=silus[h][:], in_=gates[g, c // 2][:, 2 * pair : 2 * pair + 2, c % 2 * CHUNK : (c % 2 + 1) * CHUNK], func=ACT.Silu)
+        def where(q):
+            return q // (PACK * CHUNKS), q // PACK % CHUNKS, q % PACK
 
-        def multiply(q, k):
-            g, c, pair = where(q // 2)
-            r = q % 2
-            first = (q // 2, r) not in accs
-            if first:
-                accs[q // 2, r] = psum.tile([P, 512], F32, name="bank")
-            nc.tensor.matmul_mx(
-                out=accs[q // 2, r][:],
-                lhsT=gq[g, pair, k][:, r * P : (r + 1) * P].bitcast(E5M2X4),
-                lhsT_scale=gs[g, pair, k][:, r * P : (r + 1) * P],
-                rhs=wq[c, k][:].bitcast(E4M3X4),
-                rhs_scale=ws[c, k][:],
-                start=first,
-                stop=(k == PASSES - 1),
+        def activate(q):
+            g, c, t = where(q)
+            silus[q // 2] = work.tile([P, 2, CHUNK], F32, name="silu", bufs=4)
+            nc.scalar.activation(
+                out=silus[q // 2][:],
+                in_=gates[g, c // 2][:, t : t + 2, c % 2 * CHUNK : (c % 2 + 1) * CHUNK],
+                func=ACT.Silu,
+                bias=zero_bias[:],
             )
 
-        def product(h, r):
-            g, c, pair = where(h)
-            if pair == 0 and r == 0:
-                ytiles[g, c] = work.tile([P, PACK, CHUNK], F32, name="y", bufs=3)
-            nc.vector.tensor_tensor(out=ytiles[g, c][:, 2 * pair + r, :], in0=accs[h, r][:], in1=silus[h][:, r, :], op=MULT)
+        def multiply(q, a):
+            g, c, t = where(q)
+            if a == 0:
+                sums[q] = psum.tile([P, CHUNK], F32, name="bank")
+            tokens = slice(t % 2 * P, (t % 2 + 1) * P)
+            nc.tensor.matmul_mx(
+                out=sums[q][:],
+                lhsT=g_codes[g, t // 2, a][:, tokens].bitcast(E5M2X4),
+                lhsT_scale=g_mx_scales[g, t // 2, a][:, tokens],
+                rhs=w_codes[c, a][:].bitcast(E4M3X4),
+                rhs_scale=w_mx_scales[c, a][:],
+                start=(a == 0),
+                stop=(a == PASSES - 1),
+            )
 
-        def store_y(q, n):
-            g, c, pair = where(q // 2)
-            t = slice(q % PACK + 1 - n, q % PACK + 1)
-            nc.sync.dma_start(out=y_rows[g][:, t, c * CHUNK : (c + 1) * CHUNK], in_=ytiles[g, c][:, t, :])
+        def product(q):
+            g, c, t = where(q)
+            if t == 0:
+                y_tiles[q // PACK] = work.tile([P, PACK, CHUNK], F32, name="y", bufs=3)
+            y = y_tiles[q // PACK]
+            nc.vector.tensor_tensor(out=y[:, t, :], in0=sums[q][:], in1=silus[q // 2][:, t % 2, :], op=MULT)
+            if q >= QUARTERS - 2 or t % 2 == 1:
+                tiles = slice(t if q >= QUARTERS - 2 else t - 1, t + 1)
+                nc.sync.dma_start(out=y_rows[g][:, tiles, c * CHUNK : (c + 1) * CHUNK], in_=y[:, tiles, :])
 
-        def interleave(step, engine, c0, c1):
-            g, c = divmod(step, CHUNKS)
-            if c0 == c1:
+        def interleave(s, on_vector):
+            split = CHUNK if s < CHUNKS - 1 else VECTOR_COLUMNS if s < STEPS - 1 else VECTOR_COLUMNS_LAST
+            fours = slice(0, split // 4) if on_vector else slice(split // 4, CHUNK // 4)
+            if fours.start == fours.stop:
                 return
-            if (g, c) not in ygrps:
-                ygrps[g, c] = work.tile([P, CHUNK, PACK], BF16, name="ygrp", bufs=2, align_bytes=64)
-            dst = ygrps[g, c][:].rearrange("p (c i) t -> p c t i", i=4)[:, c0 // 4 : c1 // 4]
-            src = ytiles[g, c][:].rearrange("p t (c i) -> p c t i", i=4)[:, c0 // 4 : c1 // 4]
-            if engine == "vector":
+            if s not in y_packed:
+                y_packed[s] = work.tile([P, CHUNK, PACK], BF16, name="y_packed", bufs=2, align_bytes=64)
+            dst = y_packed[s][:].rearrange("p (m i) t -> p m t i", i=4)[:, fours]
+            src = y_tiles[s][:].rearrange("p t (m i) -> p m t i", i=4)[:, fours]
+            if on_vector:
                 nc.vector.tensor_copy(out=dst, in_=src)
-            elif engine == "scalar":
-                nc.scalar.copy(out=dst, in_=src)
             else:
-                nc.gpsimd.tensor_scalar(out=dst, in0=src, scalar1=1.0, scalar2=0.0, op0=MULT, op1=ADD)
+                nc.scalar.copy(out=dst, in_=src)
 
-        def requantize(h):
-            g, c, pair = where(h)
+        def requantize(s):
+            g, c = divmod(s, CHUNKS)
             cols = slice(c * CHUNK, (c + 1) * CHUNK)
-            ycodes = work.tile([P, CHUNK], U32, name="ycodes", bufs=3, align_bytes=64)
-            nc.vector.quantize_mx(out=ycodes[:].bitcast(E4M3X4), scales=ys[g][:, cols], in_=ygrps[g, c][:].rearrange("p c t -> p (c t)"))
-            nc.sync.dma_start(out=code_rows[g][:, cols], in_=ycodes[:].bitcast(I32))
+            y_codes = work.tile([P, CHUNK], U32, name="y_codes", bufs=3, align_bytes=64)
+            nc.vector.quantize_mx(out=y_codes[:].bitcast(E4M3X4), scales=y_mx_scales[g][:, cols], in_=y_packed[s][:].rearrange("p m t -> p (m t)"))
+            nc.sync.dma_start(out=y_code_rows[g][:, cols], in_=y_codes[:].bitcast(I32))
             if c == CHUNKS - 1:
-                for q in range(4):
-                    (nc.scalar if g == GROUPS - 1 else nc.sync).dma_start(out=scale_rows[g][4 * q : 4 * q + 4, :], in_=ys[g][32 * q : 32 * q + 4, :].bitcast(I32))
+                queue = nc.scalar if g == GROUPS - 1 else nc.sync
+                for quadrant in range(P // 32):
+                    queue.dma_start(
+                        out=y_scale_rows[g][SCALE_ROWS * quadrant : SCALE_ROWS * (quadrant + 1), :],
+                        in_=y_mx_scales[g][32 * quadrant : 32 * quadrant + SCALE_ROWS, :].bitcast(I32),
+                    )
 
-        def g_units(g, pair):
-            return [("g", g, pair, k) for k in range(PASSES)]
+        def g_slabs(g, pair):
+            return [("g", g, pair, a) for a in range(PASSES)]
 
-        def w_units(c):
-            return [("w", c, pair, k) for k in range(PASSES) for pair in range(PAIRS)]
+        def w_slabs(c):
+            return [("w", c, pair, a) for a in range(PASSES) for pair in range(2)]
 
-        QUARTERS = PACK * GROUPS * CHUNKS
-        g00, g01, g1 = g_units(0, 0), g_units(0, 1), g_units(1, 0) + g_units(1, 1)
-        w0, w1 = w_units(0), w_units(1)
-        halves = [(unit, r) for unit in g1 for r in range(2)]
+        first_group = g_slabs(0, 0) + g_slabs(0, 1)
+        second_group = g_slabs(1, 0) + g_slabs(1, 1)
+        to_widen = [(slab, r) for slab in second_group for r in range(2)]
 
-        def both(unit):
-            widen(unit, 0, False)
-            widen(unit, 1, True)
+        def widen_on_both(slab):
+            widen(slab, 0, False)
+            widen(slab, 1, True)
 
-        head = [[g00[k]] + w0[2 * k : 2 * k + 2] for k in range(PASSES)] + [g01[:2] + w1[:1], g01[2:] + w1[1:3], w1[3:]]
-        passes = [[], [(0, 0)], [(0, 1)], [(0, 2)], [(2, 0), (2, 1)], [(2, 2)]]
-        to_widen = g00 + g01
-        both(to_widen[0])
-        both(to_widen[1])
-        for a, units in enumerate(head):
-            for unit in units:
-                turn(unit)
-            if a == 5:
-                product(0, 1)
-                store_y(1, 2)
-            if a > 0:
-                for unit in head[a - 1]:
-                    quantize(unit)
-            for q, k in passes[a]:
-                multiply(q, k)
-                multiply(q + 1, k)
-            if a >= 3:
-                activate(a - 3)
-            if a == 4:
-                product(0, 0)
-            if a + 2 < len(to_widen):
-                both(to_widen[a + 2])
-            if a in HVW:
-                widen(*halves.pop(0), True)
-            drain(units[0], False)
-            drain(units[1], a < HV)
-            drain(units[2], False)
-            if a in HS:
-                widen(*halves.pop(0), False)
-
-        turns = {q: [] for q in range(QUARTERS + 8)}
-        turns[3] = head[-1]
-        later = w_units(2) + w_units(3) + g1
-        for n in range(len(later) // 2):
-            turns[TQ[n]] = later[2 * n : 2 * n + 2]
-
-        for q in range(4, QUARTERS + 4):
-            for unit in turns[q]:
-                turn(unit)
-            done = (q - 4) // 4 * 2 + 1
-            if q == 4:
-                for unit in turns[3]:
-                    quantize(unit)
-                product(1, 0)
-            if halves and q in VQ:
-                widen(*halves.pop(0), True)
+        w0, rest = w_slabs(0), [first_group[3], first_group[4], w_slabs(1)[0], first_group[5]] + w_slabs(1)[1:]
+        rounds = [[first_group[a]] + w0[2 * a : 2 * a + 2] for a in range(PASSES)] + [rest[0:3], rest[3:6], rest[6:9]]
+        passes_after = [[], [(0, 0)], [(0, 1)], [(0, 2)], [(2, 0), (2, 1)], [(2, 2)]]
+        last_round = len(rounds) - 1
+        widen_on_both(first_group[0])
+        widen_on_both(first_group[1])
+        for n, slabs in enumerate(rounds):
+            for slab in slabs:
+                turn(slab)
+            if n == last_round:
+                product(1)
+            if n > 0:
+                for slab in rounds[n - 1]:
+                    quantize(slab)
+            for q, a in passes_after[n]:
+                multiply(q, a)
+                multiply(q + 1, a)
+            if n >= PASSES:
+                activate(2 * (n - PASSES))
+            if n == last_round - 1:
+                product(0)
+            if n + 2 < len(first_group):
+                widen_on_both(first_group[n + 2])
+            else:
+                widen(*to_widen.pop(0), True)
+            drain(slabs[0], False)
+            drain(slabs[1], n < last_round)
+            drain(slabs[2], False)
+        to_turn = w_slabs(2) + w_slabs(3) + second_group
+        drained = rounds[last_round]
+        for q in range(PACK, QUARTERS + 3):
+            t, finished = q % PACK, q // PACK - 1
+            slabs = [to_turn.pop(0) for n in range(2)] if to_turn and t != 3 else []
+            for slab in slabs:
+                turn(slab)
+            if q == PACK:
+                for slab in drained:
+                    quantize(slab)
+                drained = []
+                product(2)
+            if to_widen and t in (3, 0):
+                widen(*to_widen.pop(0), True)
             if q - 1 < QUARTERS:
-                product((q - 1) // 2, (q - 1) % 2)
-                if q - 1 >= QUARTERS - 2:
-                    store_y(q - 1, 1)
-                elif q % 2 == 0:
-                    store_y(q - 1, 2)
-            if q % 4 == 1 and q >= 5:
-                interleave(done // 2, "vector", 0, SH[done // 2][0])
-            if q % 4 == RQ and q >= 4 + RQ:
-                requantize(done)
-            if q > 4:
-                for unit in turns[q - 1]:
-                    quantize(unit)
+                product(q - 1)
+            if t == 1:
+                interleave(finished, True)
+            if t == 2:
+                requantize(finished)
+            for slab in drained:
+                quantize(slab)
             if q < QUARTERS:
-                for k in range(PASSES):
-                    multiply(q, k)
-            if q % 2 == 0 and q // 2 + 1 < QUARTERS // 2:
-                activate(q // 2 + 1)
-            if halves and q in SQ:
-                widen(*halves.pop(0), False)
-            for n, unit in enumerate(turns[q]):
-                drain(unit, (q, n) in DV)
-            if q % 4 == 0 and q >= 4:
-                interleave(q // 4 - 1, "scalar", SH[q // 4 - 1][0], SH[q // 4 - 1][1])
+                for a in range(PASSES):
+                    multiply(q, a)
+            if t % 2 == 0 and q + 2 < QUARTERS:
+                activate(q + 2)
+            if to_widen and t != 0:
+                widen(*to_widen.pop(0), False)
+            for slab in slabs:
+                drain(slab, False)
+            drained = slabs
+            if t == 0:
+                interleave(finished, False)

from contextlib import ExitStack

import concourse.mybir as mybir
from concourse.masks import make_identity

T, D, F = 1024, 1536, 2048
FLOPS = 2 * T * D * F

F32 = mybir.dt.float32
BF16 = mybir.dt.bfloat16
U32 = mybir.dt.uint32
I32 = mybir.dt.int32
U8 = mybir.dt.uint8
FP8 = mybir.dt.float8_e4m3fn
E4M3X4 = mybir.dt.float8_e4m3fn_x4
E5M2X4 = mybir.dt.float8_e5m2_x4
ACT = mybir.ActivationFunctionType
MULT = mybir.AluOpType.mult

P = 128
PACK = 4
K_PASS = P * PACK
PASSES = D // K_PASS
BLOCK = 32
BLOCKS = K_PASS // BLOCK
GROUPS = T // (P * PACK)
CHUNK = 512
CHUNKS = F // CHUNK
STEPS = GROUPS * CHUNKS
QUARTERS = PACK * STEPS
SCALE_ROWS = 4

VECTOR_COLUMNS = 304
VECTOR_COLUMNS_LAST = 368


def tile_swiglu_up_gradient_tokens_b13_kernel(tc, G_bytes, G_scale, w_down, gate, out_0, out_1, out_2):
    nc = tc.nc
    with ExitStack() as ctx:
        keep = ctx.enter_context(tc.tile_pool(name="keep", bufs=1))
        work = ctx.enter_context(tc.tile_pool(name="work", bufs=1))
        psum = ctx.enter_context(tc.psum_pool(name="psum", bufs=8))
        ctx.enter_context(tc.manual_schedule())

        ident = keep.tile([P, P], F32, name="ident")
        make_identity(nc, ident[:])
        zero = keep.tile([P, 1], F32, name="zero")
        nc.vector.memset(zero[:], 0.0)
        zero_bias = keep.tile([P, 1], F32, name="zero_bias")
        nc.scalar.activation(out=zero_bias[:], in_=zero[:], func=ACT.Silu)

        g_rows = G_bytes.rearrange("(g p t) k -> g p (t k)", p=P, t=PACK)
        g_scale_rows = G_scale.rearrange("(g p t) j -> g p (t j)", p=P, t=PACK)
        gate_rows = gate.rearrange("(g p t) f -> g p t f", p=P, t=PACK)
        y_rows = out_0.rearrange("(g p t) f -> g p t f", p=P, t=PACK)
        y_code_rows = out_1.rearrange("g p m t -> g p (m t)").bitcast(I32)
        y_scale_rows = out_2.bitcast(I32)

        g_scales, g_raw, w_first, w_raw, gates = {}, {}, {}, {}, {}

        def load_g_scales(g):
            g_scales[g] = keep.tile([P, PACK * D // BLOCK], F32, name="g_scales%d" % g)
            nc.sync.dma_start(out=g_scales[g][:], in_=g_scale_rows[g])

        def load_g(g, pair):
            g_raw[g, pair] = keep.tile([P, 2 * D], U8, name="g_raw%d%d" % (g, pair))
            nc.sync.dma_start(out=g_raw[g, pair][:], in_=g_rows[g][:, pair * 2 * D : (pair + 1) * 2 * D])

        def load_w_first(a):
            w_first[a] = keep.tile([P, PACK, K_PASS], BF16, name="w_first%d" % a)
            nc.sync.dma_start(out=w_first[a][:], in_=w_down[0:CHUNK, a * K_PASS : (a + 1) * K_PASS].rearrange("(r p) k -> p r k", p=P))

        def load_w(c, pair):
            w_raw[c, pair] = keep.tile([P, 2, D], BF16, name="w_raw%d%d" % (c, pair))
            row0 = c * CHUNK + pair * 2 * P
            nc.sync.dma_start(out=w_raw[c, pair][:], in_=w_down[row0 : row0 + 2 * P, :].rearrange("(p r) k -> p r k", r=2))

        def load_gate(g, half):
            gates[g, half] = keep.tile([P, PACK, 2 * CHUNK], BF16, name="gate%d%d" % (g, half))
            nc.sync.dma_start(out=gates[g, half][:], in_=gate_rows[g][:, :, half * 2 * CHUNK : (half + 1) * 2 * CHUNK])

        load_g_scales(0)
        load_g(0, 0)
        load_w_first(0)
        load_w_first(1)
        load_g(0, 1)
        load_w_first(2)
        load_w(1, 0)
        load_gate(0, 0)
        load_w(1, 1)
        load_g_scales(1)
        load_g(1, 0)
        load_w(2, 0)
        load_w(2, 1)
        load_g(1, 1)
        load_gate(0, 1)
        load_w(3, 0)
        load_w(3, 1)
        load_gate(1, 0)
        load_gate(1, 1)

        g_codes, g_mx_scales, w_codes, w_mx_scales, y_mx_scales = {}, {}, {}, {}, {}
        for g in range(GROUPS):
            y_mx_scales[g] = keep.tile([P, F], U8, name="y_mx_scales%d" % g, align_bytes=64)
            for pair in range(2):
                for a in range(PASSES):
                    g_codes[g, pair, a] = keep.tile([P, 2 * P], U32, name="g_codes%d%d%d" % (g, pair, a), align_bytes=64)
                    g_mx_scales[g, pair, a] = keep.tile([P, 2 * P], U8, name="g_mx_scales%d%d%d" % (g, pair, a), align_bytes=64)
        for c in range(CHUNKS):
            for a in range(PASSES):
                w_codes[c, a] = keep.tile([P, CHUNK], U32, name="w_codes%d%d" % (c, a), align_bytes=64)
                w_mx_scales[c, a] = keep.tile([P, CHUNK], U8, name="w_mx_scales%d%d" % (c, a), align_bytes=64)

        pair_words, turned, k_major = {}, {}, {}

        def widen(slab, r, on_vector):
            operand, g, pair, a = slab
            wide = work.tile([P, K_PASS], BF16, name="wide", bufs=2 * len(second_group), align_bytes=64)
            for j in range(BLOCKS):
                byte0 = r * D + a * K_PASS + j * BLOCK
                values = g_raw[g, pair][:, byte0 : byte0 + BLOCK].bitcast(FP8)
                column = (2 * pair + r) * (D // BLOCK) + a * BLOCKS + j
                scale = g_scales[g][:, column : column + 1]
                if on_vector:
                    by_u = wide[:].rearrange("p (u w e) -> p w u e", u=2, e=2)[:, 8 * j : 8 * j + 8]
                    nc.vector.tensor_scalar(out=by_u, in0=values.rearrange("p (w u e) -> p w u e", u=2, e=2), scalar1=scale, scalar2=None, op0=MULT)
                else:
                    nc.scalar.activation(out=wide[:, j * BLOCK : (j + 1) * BLOCK], in_=values, func=ACT.Copy, scale=scale)
            words = wide[:].bitcast(F32)
            pair_words[slab, r] = [words[:, u * P : (u + 1) * P] if on_vector else words[:, u : 2 * P : 2] for u in range(2)]

        def turn(slab):
            operand, c, pair, a = slab
            if operand == "w":
                for r in range(2):
                    rows = w_first[a][:, 2 * pair + r, :] if c == 0 else w_raw[c, pair][:, r, a * K_PASS : (a + 1) * K_PASS]
                    pair_words[slab, r] = [rows.bitcast(F32)[:, u : 2 * P : 2] for u in range(2)]
            turned[slab] = psum.tile([P, CHUNK], F32, name="bank")
            for r in range(2):
                for u in range(2):
                    nc.tensor.transpose(turned[slab][:, (2 * r + u) * P : (2 * r + u + 1) * P], pair_words[slab, r][u], ident[:])

        def drain(slab, on_vector):
            k_major[slab] = work.tile([P, 2 * K_PASS], BF16, name="k_major", bufs=6, align_bytes=64)
            order = "n r u" if slab[0] == "w" and slab[1] > 0 else "r n u"
            dst = k_major[slab][:].bitcast(F32).rearrange("p (%s) -> p %s" % (order, order), r=2, u=2)
            src = turned[slab][:].rearrange("p (r u n) -> p %s" % order, r=2, u=2)
            if on_vector:
                nc.vector.tensor_copy(out=dst, in_=src)
            else:
                nc.scalar.copy(out=dst, in_=src)

        def quantize(slab):
            operand, index, pair, a = slab
            if operand == "g":
                nc.vector.quantize_mx(out=g_codes[index, pair, a][:].bitcast(E5M2X4), scales=g_mx_scales[index, pair, a][:], in_=k_major[slab][:])
            else:
                cols = slice(pair * 2 * P, (pair + 1) * 2 * P)
                nc.vector.quantize_mx(out=w_codes[index, a][:, cols].bitcast(E4M3X4), scales=w_mx_scales[index, a][:, cols], in_=k_major[slab][:])

        sums, silus, y_tiles, y_packed = {}, {}, {}, {}

        def where(q):
            return q // (PACK * CHUNKS), q // PACK % CHUNKS, q % PACK

        def activate(q):
            g, c, t = where(q)
            silus[q // 2] = work.tile([P, 2, CHUNK], F32, name="silu", bufs=4)
            nc.scalar.activation(
                out=silus[q // 2][:],
                in_=gates[g, c // 2][:, t : t + 2, c % 2 * CHUNK : (c % 2 + 1) * CHUNK],
                func=ACT.Silu,
                bias=zero_bias[:],
            )

        def multiply(q, a):
            g, c, t = where(q)
            if a == 0:
                sums[q] = psum.tile([P, CHUNK], F32, name="bank")
            tokens = slice(t % 2 * P, (t % 2 + 1) * P)
            nc.tensor.matmul_mx(
                out=sums[q][:],
                lhsT=g_codes[g, t // 2, a][:, tokens].bitcast(E5M2X4),
                lhsT_scale=g_mx_scales[g, t // 2, a][:, tokens],
                rhs=w_codes[c, a][:].bitcast(E4M3X4),
                rhs_scale=w_mx_scales[c, a][:],
                start=(a == 0),
                stop=(a == PASSES - 1),
            )

        def product(q):
            g, c, t = where(q)
            if t == 0:
                y_tiles[q // PACK] = work.tile([P, PACK, CHUNK], F32, name="y", bufs=3)
            y = y_tiles[q // PACK]
            nc.vector.tensor_tensor(out=y[:, t, :], in0=sums[q][:], in1=silus[q // 2][:, t % 2, :], op=MULT)
            if q >= QUARTERS - 2 or t % 2 == 1:
                tiles = slice(t if q >= QUARTERS - 2 else t - 1, t + 1)
                nc.sync.dma_start(out=y_rows[g][:, tiles, c * CHUNK : (c + 1) * CHUNK], in_=y[:, tiles, :])

        def interleave(s, on_vector):
            split = CHUNK if s < CHUNKS - 1 else VECTOR_COLUMNS if s < STEPS - 1 else VECTOR_COLUMNS_LAST
            fours = slice(0, split // 4) if on_vector else slice(split // 4, CHUNK // 4)
            if fours.start == fours.stop:
                return
            if s not in y_packed:
                y_packed[s] = work.tile([P, CHUNK, PACK], BF16, name="y_packed", bufs=2, align_bytes=64)
            dst = y_packed[s][:].rearrange("p (m i) t -> p m t i", i=4)[:, fours]
            src = y_tiles[s][:].rearrange("p t (m i) -> p m t i", i=4)[:, fours]
            if on_vector:
                nc.vector.tensor_copy(out=dst, in_=src)
            else:
                nc.scalar.copy(out=dst, in_=src)

        def requantize(s):
            g, c = divmod(s, CHUNKS)
            cols = slice(c * CHUNK, (c + 1) * CHUNK)
            y_codes = work.tile([P, CHUNK], U32, name="y_codes", bufs=3, align_bytes=64)
            nc.vector.quantize_mx(out=y_codes[:].bitcast(E4M3X4), scales=y_mx_scales[g][:, cols], in_=y_packed[s][:].rearrange("p m t -> p (m t)"))
            nc.sync.dma_start(out=y_code_rows[g][:, cols], in_=y_codes[:].bitcast(I32))
            if c == CHUNKS - 1:
                queue = nc.scalar if g == GROUPS - 1 else nc.sync
                for quadrant in range(P // 32):
                    queue.dma_start(
                        out=y_scale_rows[g][SCALE_ROWS * quadrant : SCALE_ROWS * (quadrant + 1), :],
                        in_=y_mx_scales[g][32 * quadrant : 32 * quadrant + SCALE_ROWS, :].bitcast(I32),
                    )

        def g_slabs(g, pair):
            return [("g", g, pair, a) for a in range(PASSES)]

        def w_slabs(c):
            return [("w", c, pair, a) for a in range(PASSES) for pair in range(2)]

        first_group = g_slabs(0, 0) + g_slabs(0, 1)
        second_group = g_slabs(1, 0) + g_slabs(1, 1)
        to_widen = [(slab, r) for slab in second_group for r in range(2)]

        def widen_on_both(slab):
            widen(slab, 0, False)
            widen(slab, 1, True)

        w0, rest = w_slabs(0), [first_group[3], first_group[4], w_slabs(1)[0], first_group[5]] + w_slabs(1)[1:]
        rounds = [[first_group[a]] + w0[2 * a : 2 * a + 2] for a in range(PASSES)] + [rest[0:3], rest[3:6], rest[6:9]]
        passes_after = [[], [(0, 0)], [(0, 1)], [(0, 2)], [(2, 0), (2, 1)], [(2, 2)]]
        last_round = len(rounds) - 1
        widen_on_both(first_group[0])
        widen_on_both(first_group[1])
        for n, slabs in enumerate(rounds):
            for slab in slabs:
                turn(slab)
            if n == last_round:
                product(1)
            if n > 0:
                for slab in rounds[n - 1]:
                    quantize(slab)
            for q, a in passes_after[n]:
                multiply(q, a)
                multiply(q + 1, a)
            if n >= PASSES:
                activate(2 * (n - PASSES))
            if n == last_round - 1:
                product(0)
            if n + 2 < len(first_group):
                widen_on_both(first_group[n + 2])
            else:
                widen(*to_widen.pop(0), True)
            drain(slabs[0], False)
            drain(slabs[1], n < last_round)
            drain(slabs[2], False)
        to_turn = w_slabs(2) + w_slabs(3) + second_group
        drained = rounds[last_round]
        for q in range(PACK, QUARTERS + 3):
            t, finished = q % PACK, q // PACK - 1
            slabs = [to_turn.pop(0) for n in range(2)] if to_turn and t != 3 else []
            for slab in slabs:
                turn(slab)
            if q == PACK:
                for slab in drained:
                    quantize(slab)
                drained = []
                product(2)
            if to_widen and t in (3, 0):
                widen(*to_widen.pop(0), True)
            if q - 1 < QUARTERS:
                product(q - 1)
            if t == 1:
                interleave(finished, True)
            if t == 2:
                requantize(finished)
            for slab in drained:
                quantize(slab)
            if q < QUARTERS:
                for a in range(PASSES):
                    multiply(q, a)
            if t % 2 == 0 and q + 2 < QUARTERS:
                activate(q + 2)
            if to_widen and t != 0:
                widen(*to_widen.pop(0), False)
            for slab in slabs:
                drain(slab, False)
            drained = slabs
            if t == 0:
                interleave(finished, False)
